import numpy as np
import ml_dtypes


def mxq(x, axis, fmt="e4m3"):
    dtype, down = {"e4m3": (ml_dtypes.float8_e4m3fn, 7), "e5m2": (ml_dtypes.float8_e5m2, 14)}[fmt]
    v = np.moveaxis(np.asarray(x, np.float32).astype(ml_dtypes.bfloat16).astype(np.float64), axis, -1)
    blocks = v.reshape(v.shape[:-1] + (-1, 32))
    amax = np.abs(blocks).max(-1, keepdims=True)
    byte = np.maximum(np.where(amax > 0, np.frexp(amax)[1] - 1 + 127, 0) - down, 1)
    scale = np.exp2(byte - 127.0)
    codes = (blocks / scale).astype(np.float32).astype(dtype).astype(np.float64)
    return np.moveaxis((codes * scale).reshape(v.shape), -1, axis)


WIDE = False


def mx_kscale(k):
    if not WIDE:
        return np.ones(k)
    levels = np.array([30, -30])
    if k % 512:
        return np.exp2(np.random.permutation(np.resize(levels, k // 32))).repeat(32)
    a = np.empty((k // 512, 16))
    for p in range(k // 512):
        a[p, :8] = np.random.permutation(np.resize(levels, 8))
        for g in range(8):
            far = levels[np.abs(levels - a[p, g]) >= 10]
            a[p, g + 8] = far[np.random.randint(len(far))]
    return np.exp2(a.ravel()).repeat(32)


def f64(x):
    return np.asarray(x).astype(np.float64)


def striped(idx):
    return np.tile(np.asarray(idx).reshape(-1, 16).T, (8, 1)).astype(np.uint16)


def unstriped(offs):
    return offs[:16].T.reshape(-1).astype(np.int64)


E2M1 = np.array([0.0, 0.5, 1.0, 1.5, 2.0, 3.0, 4.0, 6.0, -0.0, -0.5, -1.0, -1.5, -2.0, -3.0, -4.0, -6.0])


def pack_weight(w, fmt):
    k, n = w.shape
    w = f64(np.asarray(w, np.float32).astype(ml_dtypes.bfloat16)).reshape(k // 32, 32, n)
    amax = np.abs(w).max(1)
    if fmt in ("e4m3", "e5m2"):
        byte = np.frexp(amax)[1] - 1 + 127 - (7 if fmt == "e4m3" else 14)
    else:
        mant, ex = np.frexp(amax / 6.0)
        byte = np.where(mant > 0.5, ex, ex - 1) + 127
    byte = np.clip(np.where(amax > 0, byte, 1), 1, 254)
    scaled = (w * np.exp2(127.0 - byte)[:, None, :]).reshape(k, n).astype(np.float32)
    by_word = np.ascontiguousarray(scaled.reshape(k // 512, 128, 4, n).transpose(0, 1, 3, 2))
    if fmt in ("e4m3", "e5m2"):
        words = by_word.astype(ml_dtypes.float8_e4m3fn if fmt == "e4m3" else ml_dtypes.float8_e5m2).view(np.uint8)
    else:
        c = by_word.astype(ml_dtypes.float4_e2m1fn).view(np.uint8) & 0xF
        words = (c[..., 0::2] | (c[..., 1::2] << 4)).reshape(k // 512, 128, 2 * n)
    return np.ascontiguousarray(words), np.ascontiguousarray(byte.astype(np.uint8).reshape(k // 512, 16, n))


def unpack_weight(words, scales, fmt):
    g, _, n = scales.shape
    words = np.ascontiguousarray(words).reshape(g, 128, n, -1)
    if fmt in ("e4m3", "e5m2"):
        vals = words.view(ml_dtypes.float8_e4m3fn if fmt == "e4m3" else ml_dtypes.float8_e5m2).astype(np.float64)
    else:
        nib = np.empty((g, 128, n, 4), np.uint8)
        nib[..., 0::2] = words & 0xF
        nib[..., 1::2] = words >> 4
        vals = E2M1[nib]
    vals = vals * np.repeat(np.exp2(scales.astype(np.float64) - 127.0), 8, axis=1)[..., None]
    return vals.transpose(0, 1, 3, 2).reshape(g * 512, n)


def sigmoid(v):
    return 1.0 / (1.0 + np.exp(-v))


def sgn(shape):
    return np.random.uniform(0.5, 2.0, shape) * np.where(np.random.standard_normal(shape) < 0, -1.0, 1.0)


K, T, J, R, V, C, O, N, S = 512, 1024, 256, 512, 1024, 512, 256, 256, 1024


def setup_inputs():
    n = np.random.standard_normal
    idx = np.random.permutation(V)[:R]
    idx2 = np.random.permutation(T)[:J]
    idx3 = np.random.permutation(C)[:J]
    idx4 = np.random.permutation(C)[:J]
    idx5 = np.random.permutation(C)[:O]
    idx6 = np.random.permutation(C)[:O]
    idx7 = np.random.permutation(S)[:N]
    fk = mx_kscale(K)
    fr = mx_kscale(R)
    xtp = pack_weight(n((K, T)) / fk[:, None], "e2m1")
    wtp = pack_weight(n((K, V)) * 1 / np.sqrt(K) * fk[:, None], "e4m3")
    w2p = pack_weight(n((K, R)) * 1 / np.sqrt(K) * fk[:, None], "e5m2")
    vsp = pack_weight(n((R, S)) * 1 / np.sqrt(R) / fr[:, None], "e2m1")
    return {
        "xt_words": xtp[0],
        "xt_scales": xtp[1],
        "wt_words": wtp[0],
        "wt_scales": wtp[1],
        "w2_words": w2p[0],
        "w2_scales": w2p[1],
        "sa": (np.random.uniform(0.5, 1.6, (R, 1)) * fr[:, None]).astype(np.float32),
        "sg": (sgn((R, 1))).astype(np.float32),
        "bg": (np.random.uniform(-2.0, 2.0, (R, 1))).astype(np.float32),
        "vs_words": vsp[0],
        "vs_scales": vsp[1],
        "offs": striped(idx),
        "offs2": striped(idx2),
        "offs3": striped(idx3),
        "offs4": striped(idx4),
        "offs5": striped(idx5),
        "offs6": striped(idx6),
        "offs7": striped(idx7),
    }


def reference(xt_words, xt_scales, wt_words, wt_scales, w2_words, w2_scales, sa, sg, bg, vs_words, vs_scales, offs, offs2, offs3, offs4, offs5, offs6, offs7):
    idx = unstriped(offs)
    idx2 = unstriped(offs2)
    idx3 = unstriped(offs3)
    idx4 = unstriped(offs4)
    idx5 = unstriped(offs5)
    idx6 = unstriped(offs6)
    idx7 = unstriped(offs7)
    xtu = unpack_weight(xt_words, xt_scales, "e2m1")
    wtu = unpack_weight(wt_words, wt_scales, "e4m3")
    w2u = unpack_weight(w2_words, w2_scales, "e5m2")
    vsu = unpack_weight(vs_words, vs_scales, "e2m1")
    wtidxg = wtu[:, idx]
    xtidx2g = xtu[:, idx2]
    a = wtidxg.T @ xtidx2g
    b = w2u.T @ xtidx2g
    pw = np.zeros((R, C))
    pw[:, idx3] = a
    pv = np.zeros((R, C))
    pv[:, idx4] = b
    pg = pw + pv
    hid = pg[:, idx5] * f64(sa) * sigmoid(pg[:, idx6] * f64(sg) + f64(bg))
    vsidx7g = vsu[:, idx7]
    hidq = mxq(hid, 0, "e5m2")
    y = vsidx7g.T @ hidq
    return y

@@ -1,0 +1,222 @@
+from contextlib import ExitStack
+
+import concourse.mybir as mybir
+
+K, T, J, R, V, C, O, N, S = 512, 1024, 256, 512, 1024, 512, 256, 256, 1024
+FLOPS = 2 * K * R * J * 2 + 2 * R * N * O
+
+F32 = mybir.dt.float32
+BF16 = mybir.dt.bfloat16
+I32 = mybir.dt.int32
+U32 = mybir.dt.uint32
+U16 = mybir.dt.uint16
+U8 = mybir.dt.uint8
+E4M3 = mybir.dt.float8_e4m3fn_x4
+E5M2 = mybir.dt.float8_e5m2_x4
+E2M1 = mybir.dt.float4_e2m1fn_x4
+ACT = mybir.ActivationFunctionType
+ALU = mybir.AluOpType
+
+P = 128
+PACK = 4
+QUADS = 4
+HALF = O // 2
+
+
+def tile_list_gatedshared_storeleads_store_plain_kernel(
+    tc, xt_words, xt_scales, wt_words, wt_scales, w2_words, w2_scales, sa, sg, bg,
+    vs_words, vs_scales, offs, offs2, offs3, offs4, offs5, offs6, offs7, out,
+):
+    nc = tc.nc
+    with ExitStack() as ctx:
+        keep = ctx.enter_context(tc.tile_pool(name="keep", bufs=1))
+        psum = ctx.enter_context(tc.psum_pool(name="psum", bufs=1))
+
+        def sb(shape, dtype, name):
+            return keep.tile(shape, dtype, name=name, align_bytes=64)
+
+        def load_list(src, name):
+            tile = sb([P, src.shape[1]], U16, name)
+            nc.sync.dma_start(tile[:], src)
+            return tile
+
+        def load_words(queue, src, shape, dtype, name):
+            tile = sb(shape, dtype, name)
+            queue.dma_start(tile[:].bitcast(I32), src.bitcast(I32))
+            return tile
+
+        def zeroed_plane(width, name):
+            tile = sb([P, width], U8, name)
+            nc.vector.memset(tile[:].bitcast(I32), 0)
+            return tile
+
+        def load_staged_scales(src, name):
+            width = src.shape[2]
+            tile = sb([PACK, QUADS, width], U8, name)
+            nc.sync.dma_start(tile[:].bitcast(I32), src[0].rearrange("(q r) n -> r q n", r=PACK).bitcast(I32))
+            return tile
+
+        def spread_scales(plane, staged):
+            for q in range(QUADS):
+                nc.vector.tensor_copy(plane[32 * q : 32 * q + PACK, :].bitcast(I32), staged[:, q, :].bitcast(I32))
+
+        def load_scales_in_place(plane, src):
+            for q in range(QUADS):
+                nc.sync.dma_start(
+                    plane[32 * q : 32 * q + PACK, :].bitcast(I32), src[0, PACK * q : PACK * (q + 1), :].bitcast(I32)
+                )
+
+        def load_rows(src, name):
+            tile = sb([P, PACK], F32, name)
+            nc.sync.dma_start(tile[:], src.rearrange("(p t) one -> p (t one)", t=PACK))
+            return tile
+
+        xt_plane = zeroed_plane(T, "xt_plane")
+        w2_plane = zeroed_plane(R, "w2_plane")
+        wt_plane = zeroed_plane(V, "wt_plane")
+        vs_plane = zeroed_plane(S, "vs_plane")
+
+        xt_table = load_words(nc.scalar, xt_words[0], [P, T], U16, "xt_table")
+        w2_loaded = load_words(nc.scalar, w2_words[0].rearrange("p n t -> p (n t)"), [P, R], U32, "w2_loaded")
+        w2_staged = load_staged_scales(w2_scales, "w2_staged")
+        token_list = load_list(offs2, "token_list")
+        load_scales_in_place(xt_plane, xt_scales)
+        wt_table = load_words(nc.sync, wt_words[0].rearrange("p n t -> p (n t)"), [P, V], U32, "wt_table")
+        feature_list = load_list(offs, "feature_list")
+        load_scales_in_place(wt_plane, wt_scales)
+        b_places = load_list(offs4, "b_places")
+        a_places = load_list(offs3, "a_places")
+        output_list = load_list(offs7, "output_list")
+        load_scales_in_place(vs_plane, vs_scales)
+        vs_table = load_words(nc.sync, vs_words[0], [P, S], U16, "vs_table")
+        weight = load_rows(sa, "weight")
+        slope = load_rows(sg, "slope")
+        offset = load_rows(bg, "offset")
+        value_list = load_list(offs5, "value_list")
+        gate_list = load_list(offs6, "gate_list")
+
+        spread_scales(w2_plane, w2_staged)
+        w2_scale = sb([P, PACK, P], U8, "w2_scale")
+        nc.vector.tensor_copy(w2_scale[:], w2_plane[:].rearrange("p (m t) -> p t m", t=PACK))
+        x_scale = sb([P, J], U8, "x_scale")
+        nc.vector.tensor_copy(x_scale[:], xt_plane[:].indirect(token_list[:]))
+        w2_code = sb([P, PACK, P], U32, "w2_code")
+        nc.scalar.copy(w2_code[:], w2_loaded[:].rearrange("p (m t) -> p t m", t=PACK))
+        x_code = sb([P, J], U16, "x_code")
+        nc.vector.tensor_copy(x_code[:], xt_table[:].indirect(token_list[:]))
+
+        a_boards = [sb([P, C], F32, "a_board%d" % i) for i in range(2)]
+        b_boards = [sb([P, C], F32, "b_board%d" % t) for t in range(PACK)]
+        for board in (b_boards[0], b_boards[1], a_boards[0], a_boards[1], b_boards[2], b_boards[3]):
+            nc.vector.memset(board[:], 0.0)
+
+        wt_code = sb([P, PACK, P], U32, "wt_code")
+        wt_scale = sb([P, PACK, P], U8, "wt_scale")
+        stationary = {"a": (wt_code, wt_scale, E4M3), "b": (w2_code, w2_scale, E5M2)}
+        rows_of = {}
+
+        def first_stage(*members):
+            name = "".join("%s%d" % m for m in members)
+            bank = psum.tile([P, len(members), J], F32, name="bank_" + name)
+            rows = sb([P, len(members), J], F32, "rows_" + name)
+            for i, (which, t) in enumerate(members):
+                code, scale, fmt = stationary[which]
+                nc.tensor.matmul_mx(
+                    bank[:, i, :], lhsT=code[:, t, :].bitcast(fmt), lhsT_scale=scale[:, t, :],
+                    rhs=x_code[:].bitcast(E2M1), rhs_scale=x_scale[:], start=True, stop=True,
+                )
+                rows_of[which, t] = rows[:, i, :]
+            return rows, bank
+
+        b0 = first_stage(("b", 0))
+        b1 = first_stage(("b", 1))
+        nc.vector.tensor_copy(wt_code[:].rearrange("p t m -> p m t"), wt_table[:].indirect(feature_list[:]))
+        nc.vector.tensor_copy(wt_scale[:].rearrange("p t m -> p m t"), wt_plane[:].indirect(feature_list[:]))
+        a0 = first_stage(("a", 0))
+        a1b2 = first_stage(("a", 1), ("b", 2))
+        a2b3 = first_stage(("a", 2), ("b", 3))
+        a3 = first_stage(("a", 3))
+
+        boards = [sb([P, C], F32, "board%d" % t) for t in range(PACK)]
+        values = sb([P, PACK, O], F32, "values")
+        gates = sb([P, PACK, O], F32, "gates")
+
+        def put_b(t):
+            nc.scalar.activation(b_boards[t][:].indirect(b_places[:]), rows_of["b", t], ACT.Copy)
+
+        def put_a(t):
+            nc.vector.tensor_copy(a_boards[t % 2][:].indirect(a_places[:]), rows_of["a", t])
+
+        def join(t):
+            nc.vector.tensor_tensor(boards[t][:], a_boards[t % 2][:], b_boards[t][:], ALU.add)
+
+        def look(t, lo, hi):
+            cols = slice(lo // 16, hi // 16)
+            nc.scalar.activation(
+                values[:, t, lo:hi], boards[t][:].indirect(value_list[:, cols]), ACT.Copy, scale=weight[:, t : t + 1]
+            )
+            nc.scalar.activation(
+                gates[:, t, lo:hi], boards[t][:].indirect(gate_list[:, cols]), ACT.Sigmoid,
+                bias=offset[:, t : t + 1], scale=slope[:, t : t + 1],
+            )
+
+        v_code = sb([P, N], U16, "v_code")
+        v_scale = sb([P, N], U8, "v_scale")
+
+        nc.scalar.copy(b0[0][:], b0[1][:])
+        put_b(0)
+        nc.scalar.copy(b1[0][:], b1[1][:])
+        put_b(1)
+        nc.vector.tensor_copy(v_scale[:], vs_plane[:].indirect(output_list[:]))
+        nc.vector.tensor_copy(a0[0][:], a0[1][:])
+        put_a(0)
+        nc.scalar.copy(a1b2[0][:], a1b2[1][:])
+        nc.scalar.copy(a2b3[0][:], a2b3[1][:])
+        nc.scalar.copy(a3[0][:], a3[1][:])
+        put_b(2)
+        put_b(3)
+        put_a(1)
+        join(0)
+        look(0, 0, O)
+        put_a(2)
+        join(1)
+        join(2)
+        look(1, 0, O)
+        put_a(3)
+        look(2, 0, O)
+        join(3)
+        nc.vector.tensor_copy(v_code[:], vs_table[:].indirect(output_list[:]))
+
+        for h in range(2):
+            look(3, h * HALF, (h + 1) * HALF)
+        out_banks = ("bank_b0", "bank_b1", "bank_y0", "bank_y1")
+        hidden = []
+        for h in range(2):
+            cols = slice(h * HALF, (h + 1) * HALF)
+            tile = sb([P, HALF, PACK], BF16, "hidden%d" % h)
+            nc.vector.tensor_tensor(
+                tile[:].rearrange("p (c i) t -> p c t i", i=4),
+                values[:, :, cols].rearrange("p t (c i) -> p c t i", i=4),
+                gates[:, :, cols].rearrange("p t (c i) -> p c t i", i=4),
+                ALU.mult,
+            )
+            hidden.append(tile)
+        for h in range(2):
+            cols = slice(h * HALF, (h + 1) * HALF)
+            h_code = sb([P, HALF], U32, "h_code%d" % h)
+            h_scale = sb([P, HALF], U8, "h_scale%d" % h)
+            nc.vector.quantize_mx(h_code[:].bitcast(E5M2), h_scale[:], hidden[h][:].rearrange("p o t -> p (o t)"))
+            for n in range(N // P):
+                rows = slice(n * P, (n + 1) * P)
+                bank = psum.tile([P, HALF], F32, name=out_banks[2 * h + n])
+                nc.tensor.matmul_mx(
+                    bank[:], lhsT=v_code[:, rows].bitcast(E2M1), lhsT_scale=v_scale[:, rows],
+                    rhs=h_code[:].bitcast(E5M2), rhs_scale=h_scale[:], start=True, stop=True,
+                )
+                result = sb([P, HALF], F32, "result%d%d" % (h, n))
+                if n == 0:
+                    nc.scalar.copy(result[:], bank[:])
+                    nc.scalar.dma_start(out[rows, cols], result[:])
+                else:
+                    nc.vector.tensor_copy(result[:], bank[:])
+                    nc.sync.dma_start(out[rows, cols], result[:])

@@ -75,6 +75,10 @@ def tile_list_gatedshared_storeleads_store_plain_kernel(
         w2_plane = zeroed_plane(R, "w2_plane")
         wt_plane = zeroed_plane(V, "wt_plane")
         vs_plane = zeroed_plane(S, "vs_plane")
+        seed = sb([P, 1], F32, "seed")
+        nc.gpsimd.memset(seed[:], 0.0)
+        primer = sb([P, 1], F32, "primer")
+        nc.scalar.activation(primer[:], seed[:], ACT.Sigmoid)
 
         xt_table = load_words(nc.scalar, xt_words[0], [P, T], U16, "xt_table")
         w2_loaded = load_words(nc.scalar, w2_words[0].rearrange("p n t -> p (n t)"), [P, R], U32, "w2_loaded")

@@ -45,9 +45,9 @@ def tile_list_gatedshared_storeleads_store_plain_kernel(
             queue.dma_start(tile[:].bitcast(I32), src.bitcast(I32))
             return tile
 
-        def zeroed_plane(width, name):
+        def zeroed_plane(engine, width, name):
             tile = sb([P, width], U8, name)
-            nc.vector.memset(tile[:].bitcast(I32), 0)
+            engine.memset(tile[:].bitcast(I32), 0)
             return tile
 
         def load_staged_scales(src, name):
@@ -60,9 +60,9 @@ def tile_list_gatedshared_storeleads_store_plain_kernel(
             for q in range(QUADS):
                 nc.vector.tensor_copy(plane[32 * q : 32 * q + PACK, :].bitcast(I32), staged[:, q, :].bitcast(I32))
 
-        def load_scales_in_place(plane, src):
+        def load_scales_in_place(queue, plane, src):
             for q in range(QUADS):
-                nc.sync.dma_start(
+                queue.dma_start(
                     plane[32 * q : 32 * q + PACK, :].bitcast(I32), src[0, PACK * q : PACK * (q + 1), :].bitcast(I32)
                 )
 
@@ -71,33 +71,33 @@ def tile_list_gatedshared_storeleads_store_plain_kernel(
             nc.sync.dma_start(tile[:], src.rearrange("(p t) one -> p (t one)", t=PACK))
             return tile
 
-        xt_plane = zeroed_plane(T, "xt_plane")
-        w2_plane = zeroed_plane(R, "w2_plane")
-        wt_plane = zeroed_plane(V, "wt_plane")
-        vs_plane = zeroed_plane(S, "vs_plane")
+        xt_plane = zeroed_plane(nc.vector, T, "xt_plane")
+        w2_plane = zeroed_plane(nc.vector, R, "w2_plane")
+        wt_plane = zeroed_plane(nc.vector, V, "wt_plane")
         seed = sb([P, 1], F32, "seed")
         nc.gpsimd.memset(seed[:], 0.0)
         primer = sb([P, 1], F32, "primer")
         nc.scalar.activation(primer[:], seed[:], ACT.Sigmoid)
+        vs_plane = zeroed_plane(nc.gpsimd, S, "vs_plane")
 
         xt_table = load_words(nc.scalar, xt_words[0], [P, T], U16, "xt_table")
         w2_loaded = load_words(nc.scalar, w2_words[0].rearrange("p n t -> p (n t)"), [P, R], U32, "w2_loaded")
         w2_staged = load_staged_scales(w2_scales, "w2_staged")
         token_list = load_list(offs2, "token_list")
-        load_scales_in_place(xt_plane, xt_scales)
+        load_scales_in_place(nc.sync, xt_plane, xt_scales)
         wt_table = load_words(nc.sync, wt_words[0].rearrange("p n t -> p (n t)"), [P, V], U32, "wt_table")
         feature_list = load_list(offs, "feature_list")
-        load_scales_in_place(wt_plane, wt_scales)
+        load_scales_in_place(nc.sync, wt_plane, wt_scales)
         b_places = load_list(offs4, "b_places")
-        a_places = load_list(offs3, "a_places")
-        output_list = load_list(offs7, "output_list")
-        load_scales_in_place(vs_plane, vs_scales)
-        vs_table = load_words(nc.sync, vs_words[0], [P, S], U16, "vs_table")
         weight = load_rows(sa, "weight")
         slope = load_rows(sg, "slope")
         offset = load_rows(bg, "offset")
         value_list = load_list(offs5, "value_list")
         gate_list = load_list(offs6, "gate_list")
+        a_places = load_list(offs3, "a_places")
+        output_list = load_list(offs7, "output_list")
+        load_scales_in_place(nc.gpsimd, vs_plane, vs_scales)
+        vs_table = load_words(nc.sync, vs_words[0], [P, S], U16, "vs_table")
 
         spread_scales(w2_plane, w2_staged)
         w2_scale = sb([P, PACK, P], U8, "w2_scale")
@@ -134,14 +134,17 @@ def tile_list_gatedshared_storeleads_store_plain_kernel(
 
         b0 = first_stage(("b", 0))
         b1 = first_stage(("b", 1))
+        b23 = first_stage(("b", 2), ("b", 3))
         nc.vector.tensor_copy(wt_code[:].rearrange("p t m -> p m t"), wt_table[:].indirect(feature_list[:]))
         nc.vector.tensor_copy(wt_scale[:].rearrange("p t m -> p m t"), wt_plane[:].indirect(feature_list[:]))
+        v_scale = sb([P, N], U8, "v_scale")
+        nc.vector.tensor_copy(v_scale[:], vs_plane[:].indirect(output_list[:]))
         a0 = first_stage(("a", 0))
-        a1b2 = first_stage(("a", 1), ("b", 2))
-        a2b3 = first_stage(("a", 2), ("b", 3))
-        a3 = first_stage(("a", 3))
+        a1 = first_stage(("a", 1))
+        a23 = first_stage(("a", 2), ("a", 3))
 
-        boards = [sb([P, C], F32, "board%d" % t) for t in range(PACK)]
+        boards = [sb([P, C], F32, "board%d" % i) for i in range(3)]
+        boards.append(boards[1])
         values = sb([P, PACK, O], F32, "values")
         gates = sb([P, PACK, O], F32, "gates")
 
@@ -151,8 +154,8 @@ def tile_list_gatedshared_storeleads_store_plain_kernel(
         def put_a(t):
             nc.vector.tensor_copy(a_boards[t % 2][:].indirect(a_places[:]), rows_of["a", t])
 
-        def join(t):
-            nc.vector.tensor_tensor(boards[t][:], a_boards[t % 2][:], b_boards[t][:], ALU.add)
+        def join(engine, t):
+            engine.tensor_tensor(boards[t][:], a_boards[t % 2][:], b_boards[t][:], ALU.add)
 
         def look(t, lo, hi):
             cols = slice(lo // 16, hi // 16)
@@ -164,32 +167,30 @@ def tile_list_gatedshared_storeleads_store_plain_kernel(
                 bias=offset[:, t : t + 1], scale=slope[:, t : t + 1],
             )
 
-        v_code = sb([P, N], U16, "v_code")
-        v_scale = sb([P, N], U8, "v_scale")
 
         nc.scalar.copy(b0[0][:], b0[1][:])
-        put_b(0)
         nc.scalar.copy(b1[0][:], b1[1][:])
+        put_b(0)
+        nc.scalar.copy(b23[0][:], b23[1][:])
         put_b(1)
-        nc.vector.tensor_copy(v_scale[:], vs_plane[:].indirect(output_list[:]))
-        nc.vector.tensor_copy(a0[0][:], a0[1][:])
-        put_a(0)
-        nc.scalar.copy(a1b2[0][:], a1b2[1][:])
-        nc.scalar.copy(a2b3[0][:], a2b3[1][:])
-        nc.scalar.copy(a3[0][:], a3[1][:])
         put_b(2)
         put_b(3)
+        nc.vector.tensor_copy(a0[0][:], a0[1][:])
+        nc.vector.tensor_copy(a1[0][:], a1[1][:])
+        put_a(0)
+        join(nc.gpsimd, 0)
+        nc.vector.tensor_copy(a23[0][:], a23[1][:])
         put_a(1)
-        join(0)
-        look(0, 0, O)
+        join(nc.gpsimd, 1)
         put_a(2)
-        join(1)
-        join(2)
-        look(1, 0, O)
+        look(0, 0, O)
+        join(nc.gpsimd, 2)
         put_a(3)
-        look(2, 0, O)
-        join(3)
+        look(1, 0, O)
+        v_code = sb([P, N], U16, "v_code")
         nc.vector.tensor_copy(v_code[:], vs_table[:].indirect(output_list[:]))
+        join(nc.vector, 3)
+        look(2, 0, O)
 
         for h in range(2):
             look(3, h * HALF, (h + 1) * HALF)

@@ -60,8 +60,8 @@ def tile_list_gatedshared_storeleads_store_plain_kernel(
             for q in range(QUADS):
                 nc.vector.tensor_copy(plane[32 * q : 32 * q + PACK, :].bitcast(I32), staged[:, q, :].bitcast(I32))
 
-        def load_scales_in_place(queue, plane, src):
-            for q in range(QUADS):
+        def load_scales_in_place(queues, plane, src):
+            for q, queue in enumerate(queues):
                 queue.dma_start(
                     plane[32 * q : 32 * q + PACK, :].bitcast(I32), src[0, PACK * q : PACK * (q + 1), :].bitcast(I32)
                 )
@@ -74,20 +74,20 @@ def tile_list_gatedshared_storeleads_store_plain_kernel(
         xt_plane = zeroed_plane(nc.vector, T, "xt_plane")
         w2_plane = zeroed_plane(nc.vector, R, "w2_plane")
         wt_plane = zeroed_plane(nc.vector, V, "wt_plane")
+        vs_plane = zeroed_plane(nc.vector, S, "vs_plane")
         seed = sb([P, 1], F32, "seed")
         nc.gpsimd.memset(seed[:], 0.0)
         primer = sb([P, 1], F32, "primer")
         nc.scalar.activation(primer[:], seed[:], ACT.Sigmoid)
-        vs_plane = zeroed_plane(nc.gpsimd, S, "vs_plane")
 
         xt_table = load_words(nc.scalar, xt_words[0], [P, T], U16, "xt_table")
         w2_loaded = load_words(nc.scalar, w2_words[0].rearrange("p n t -> p (n t)"), [P, R], U32, "w2_loaded")
         w2_staged = load_staged_scales(w2_scales, "w2_staged")
         token_list = load_list(offs2, "token_list")
-        load_scales_in_place(nc.sync, xt_plane, xt_scales)
+        load_scales_in_place([nc.sync, nc.scalar] * 2, xt_plane, xt_scales)
         wt_table = load_words(nc.sync, wt_words[0].rearrange("p n t -> p (n t)"), [P, V], U32, "wt_table")
         feature_list = load_list(offs, "feature_list")
-        load_scales_in_place(nc.sync, wt_plane, wt_scales)
+        load_scales_in_place([nc.sync] * QUADS, wt_plane, wt_scales)
         b_places = load_list(offs4, "b_places")
         weight = load_rows(sa, "weight")
         slope = load_rows(sg, "slope")
@@ -96,12 +96,14 @@ def tile_list_gatedshared_storeleads_store_plain_kernel(
         gate_list = load_list(offs6, "gate_list")
         a_places = load_list(offs3, "a_places")
         output_list = load_list(offs7, "output_list")
-        load_scales_in_place(nc.gpsimd, vs_plane, vs_scales)
+        load_scales_in_place([nc.sync] * QUADS, vs_plane, vs_scales)
         vs_table = load_words(nc.sync, vs_words[0], [P, S], U16, "vs_table")
 
         spread_scales(w2_plane, w2_staged)
         w2_scale = sb([P, PACK, P], U8, "w2_scale")
-        nc.vector.tensor_copy(w2_scale[:], w2_plane[:].rearrange("p (m t) -> p t m", t=PACK))
+        w2_dealt = w2_plane[:].rearrange("p (m t) -> p t m", t=PACK)
+        nc.vector.tensor_copy(w2_scale[:, 0:2, :], w2_dealt[:, 0:2, :])
+        nc.gpsimd.tensor_copy(w2_scale[:, 2:4, :], w2_dealt[:, 2:4, :])
         x_scale = sb([P, J], U8, "x_scale")
         nc.vector.tensor_copy(x_scale[:], xt_plane[:].indirect(token_list[:]))
         w2_code = sb([P, PACK, P], U32, "w2_code")
@@ -137,8 +139,6 @@ def tile_list_gatedshared_storeleads_store_plain_kernel(
         b23 = first_stage(("b", 2), ("b", 3))
         nc.vector.tensor_copy(wt_code[:].rearrange("p t m -> p m t"), wt_table[:].indirect(feature_list[:]))
         nc.vector.tensor_copy(wt_scale[:].rearrange("p t m -> p m t"), wt_plane[:].indirect(feature_list[:]))
-        v_scale = sb([P, N], U8, "v_scale")
-        nc.vector.tensor_copy(v_scale[:], vs_plane[:].indirect(output_list[:]))
         a0 = first_stage(("a", 0))
         a1 = first_stage(("a", 1))
         a23 = first_stage(("a", 2), ("a", 3))
@@ -187,10 +187,12 @@ def tile_list_gatedshared_storeleads_store_plain_kernel(
         join(nc.gpsimd, 2)
         put_a(3)
         look(1, 0, O)
-        v_code = sb([P, N], U16, "v_code")
-        nc.vector.tensor_copy(v_code[:], vs_table[:].indirect(output_list[:]))
+        v_scale = sb([P, N], U8, "v_scale")
+        nc.vector.tensor_copy(v_scale[:], vs_plane[:].indirect(output_list[:]))
         join(nc.vector, 3)
         look(2, 0, O)
+        v_code = sb([P, N], U16, "v_code")
+        nc.vector.tensor_copy(v_code[:], vs_table[:].indirect(output_list[:]))
 
         for h in range(2):
             look(3, h * HALF, (h + 1) * HALF)

@@ -20,7 +20,11 @@ ALU = mybir.AluOpType
 P = 128
 PACK = 4
 QUADS = 4
+QUAD_ROWS = 4
+PER_COLUMN = 16
+RUN = 4
 HALF = O // 2
+LAST = PACK - 1
 
 
 def tile_list_gatedshared_storeleads_store_plain_kernel(
@@ -45,53 +49,48 @@ def tile_list_gatedshared_storeleads_store_plain_kernel(
             queue.dma_start(tile[:].bitcast(I32), src.bitcast(I32))
             return tile
 
-        def zeroed_plane(engine, width, name):
+        def zeroed_plane(width, name):
             tile = sb([P, width], U8, name)
-            engine.memset(tile[:].bitcast(I32), 0)
+            nc.vector.memset(tile[:].bitcast(I32), 0)
             return tile
 
-        def load_staged_scales(src, name):
-            width = src.shape[2]
-            tile = sb([PACK, QUADS, width], U8, name)
-            nc.sync.dma_start(tile[:].bitcast(I32), src[0].rearrange("(q r) n -> r q n", r=PACK).bitcast(I32))
-            return tile
-
-        def spread_scales(plane, staged):
-            for q in range(QUADS):
-                nc.vector.tensor_copy(plane[32 * q : 32 * q + PACK, :].bitcast(I32), staged[:, q, :].bitcast(I32))
+        def live_rows(plane, q):
+            return plane[32 * q : 32 * q + QUAD_ROWS, :].bitcast(I32)
 
         def load_scales_in_place(queues, plane, src):
             for q, queue in enumerate(queues):
-                queue.dma_start(
-                    plane[32 * q : 32 * q + PACK, :].bitcast(I32), src[0, PACK * q : PACK * (q + 1), :].bitcast(I32)
-                )
+                queue.dma_start(live_rows(plane, q), src[0, QUAD_ROWS * q : QUAD_ROWS * (q + 1), :].bitcast(I32))
 
-        def load_rows(src, name):
+        def load_per_row(src, name):
             tile = sb([P, PACK], F32, name)
             nc.sync.dma_start(tile[:], src.rearrange("(p t) one -> p (t one)", t=PACK))
             return tile
 
-        xt_plane = zeroed_plane(nc.vector, T, "xt_plane")
-        w2_plane = zeroed_plane(nc.vector, R, "w2_plane")
-        wt_plane = zeroed_plane(nc.vector, V, "wt_plane")
-        vs_plane = zeroed_plane(nc.vector, S, "vs_plane")
+        xt_plane = zeroed_plane(T, "xt_plane")
+        w2_plane = zeroed_plane(R, "w2_plane")
+        wt_plane = zeroed_plane(V, "wt_plane")
+        vs_plane = zeroed_plane(S, "vs_plane")
+
         seed = sb([P, 1], F32, "seed")
         nc.gpsimd.memset(seed[:], 0.0)
         primer = sb([P, 1], F32, "primer")
         nc.scalar.activation(primer[:], seed[:], ACT.Sigmoid)
 
-        xt_table = load_words(nc.scalar, xt_words[0], [P, T], U16, "xt_table")
         w2_loaded = load_words(nc.scalar, w2_words[0].rearrange("p n t -> p (n t)"), [P, R], U32, "w2_loaded")
-        w2_staged = load_staged_scales(w2_scales, "w2_staged")
+        xt_table = load_words(nc.scalar, xt_words[0], [P, T], U16, "xt_table")
+        w2_staged = sb([QUAD_ROWS, QUADS, R], U8, "w2_staged")
+        nc.sync.dma_start(
+            w2_staged[:].bitcast(I32), w2_scales[0].rearrange("(q i) n -> i q n", i=QUAD_ROWS).bitcast(I32)
+        )
         token_list = load_list(offs2, "token_list")
         load_scales_in_place([nc.sync, nc.scalar] * 2, xt_plane, xt_scales)
         wt_table = load_words(nc.sync, wt_words[0].rearrange("p n t -> p (n t)"), [P, V], U32, "wt_table")
         feature_list = load_list(offs, "feature_list")
         load_scales_in_place([nc.sync] * QUADS, wt_plane, wt_scales)
         b_places = load_list(offs4, "b_places")
-        weight = load_rows(sa, "weight")
-        slope = load_rows(sg, "slope")
-        offset = load_rows(bg, "offset")
+        weight = load_per_row(sa, "weight")
+        slope = load_per_row(sg, "slope")
+        offset = load_per_row(bg, "offset")
         value_list = load_list(offs5, "value_list")
         gate_list = load_list(offs6, "gate_list")
         a_places = load_list(offs3, "a_places")
@@ -99,21 +98,26 @@ def tile_list_gatedshared_storeleads_store_plain_kernel(
         load_scales_in_place([nc.sync] * QUADS, vs_plane, vs_scales)
         vs_table = load_words(nc.sync, vs_words[0], [P, S], U16, "vs_table")
 
-        spread_scales(w2_plane, w2_staged)
+        for q in range(QUADS):
+            nc.vector.tensor_copy(live_rows(w2_plane, q), w2_staged[:, q, :].bitcast(I32))
         w2_scale = sb([P, PACK, P], U8, "w2_scale")
-        w2_dealt = w2_plane[:].rearrange("p (m t) -> p t m", t=PACK)
-        nc.vector.tensor_copy(w2_scale[:, 0:2, :], w2_dealt[:, 0:2, :])
-        nc.gpsimd.tensor_copy(w2_scale[:, 2:4, :], w2_dealt[:, 2:4, :])
+        w2_plane_by_slice = w2_plane[:].rearrange("p (m t) -> p t m", t=PACK)
+        nc.vector.tensor_copy(w2_scale[:, 0:2, :], w2_plane_by_slice[:, 0:2, :])
+        nc.gpsimd.tensor_copy(w2_scale[:, 2:4, :], w2_plane_by_slice[:, 2:4, :])
         x_scale = sb([P, J], U8, "x_scale")
         nc.vector.tensor_copy(x_scale[:], xt_plane[:].indirect(token_list[:]))
         w2_code = sb([P, PACK, P], U32, "w2_code")
-        nc.scalar.copy(w2_code[:], w2_loaded[:].rearrange("p (m t) -> p t m", t=PACK))
+        for pair in (slice(0, 2), slice(2, 4)):
+            nc.scalar.copy(
+                w2_code[:, pair, :].rearrange("p t m -> p m t"),
+                w2_loaded[:].rearrange("p (m t) -> p m t", t=PACK)[:, :, pair],
+            )
         x_code = sb([P, J], U16, "x_code")
         nc.vector.tensor_copy(x_code[:], xt_table[:].indirect(token_list[:]))
 
         a_boards = [sb([P, C], F32, "a_board%d" % i) for i in range(2)]
         b_boards = [sb([P, C], F32, "b_board%d" % t) for t in range(PACK)]
-        for board in (b_boards[0], b_boards[1], a_boards[0], a_boards[1], b_boards[2], b_boards[3]):
+        for board in b_boards[:2] + a_boards + b_boards[2:]:
             nc.vector.memset(board[:], 0.0)
 
         wt_code = sb([P, PACK, P], U32, "wt_code")
@@ -121,29 +125,29 @@ def tile_list_gatedshared_storeleads_store_plain_kernel(
         stationary = {"a": (wt_code, wt_scale, E4M3), "b": (w2_code, w2_scale, E5M2)}
         rows_of = {}
 
-        def first_stage(*members):
-            name = "".join("%s%d" % m for m in members)
-            bank = psum.tile([P, len(members), J], F32, name="bank_" + name)
-            rows = sb([P, len(members), J], F32, "rows_" + name)
-            for i, (which, t) in enumerate(members):
-                code, scale, fmt = stationary[which]
+        def first_stage(which, *slices):
+            name = "".join("%s%d" % (which, t) for t in slices)
+            code, scale, fmt = stationary[which]
+            bank = psum.tile([P, len(slices), J], F32, name="bank_" + name)
+            rows = sb([P, len(slices), J], F32, "rows_" + name)
+            for i, t in enumerate(slices):
                 nc.tensor.matmul_mx(
                     bank[:, i, :], lhsT=code[:, t, :].bitcast(fmt), lhsT_scale=scale[:, t, :],
                     rhs=x_code[:].bitcast(E2M1), rhs_scale=x_scale[:], start=True, stop=True,
                 )
                 rows_of[which, t] = rows[:, i, :]
-            return rows, bank
+            return rows[:], bank[:]
 
-        b0 = first_stage(("b", 0))
-        b1 = first_stage(("b", 1))
-        b23 = first_stage(("b", 2), ("b", 3))
+        b0 = first_stage("b", 0)
+        b1 = first_stage("b", 1)
+        b23 = first_stage("b", 2, 3)
         nc.vector.tensor_copy(wt_code[:].rearrange("p t m -> p m t"), wt_table[:].indirect(feature_list[:]))
         nc.vector.tensor_copy(wt_scale[:].rearrange("p t m -> p m t"), wt_plane[:].indirect(feature_list[:]))
-        a0 = first_stage(("a", 0))
-        a1 = first_stage(("a", 1))
-        a23 = first_stage(("a", 2), ("a", 3))
+        a0 = first_stage("a", 0)
+        a1 = first_stage("a", 1)
+        a23 = first_stage("a", 2, 3)
 
-        boards = [sb([P, C], F32, "board%d" % i) for i in range(3)]
+        boards = [sb([P, C], F32, "board%d" % t) for t in range(LAST)]
         boards.append(boards[1])
         values = sb([P, PACK, O], F32, "values")
         gates = sb([P, PACK, O], F32, "gates")
@@ -158,72 +162,70 @@ def tile_list_gatedshared_storeleads_store_plain_kernel(
             engine.tensor_tensor(boards[t][:], a_boards[t % 2][:], b_boards[t][:], ALU.add)
 
         def look(t, lo, hi):
-            cols = slice(lo // 16, hi // 16)
+            entries = slice(lo // PER_COLUMN, hi // PER_COLUMN)
             nc.scalar.activation(
-                values[:, t, lo:hi], boards[t][:].indirect(value_list[:, cols]), ACT.Copy, scale=weight[:, t : t + 1]
+                values[:, t, lo:hi], boards[t][:].indirect(value_list[:, entries]), ACT.Copy,
+                scale=weight[:, t : t + 1],
             )
             nc.scalar.activation(
-                gates[:, t, lo:hi], boards[t][:].indirect(gate_list[:, cols]), ACT.Sigmoid,
+                gates[:, t, lo:hi], boards[t][:].indirect(gate_list[:, entries]), ACT.Sigmoid,
                 bias=offset[:, t : t + 1], scale=slope[:, t : t + 1],
             )
 
-
-        nc.scalar.copy(b0[0][:], b0[1][:])
-        nc.scalar.copy(b1[0][:], b1[1][:])
+        nc.scalar.copy(*b0)
+        nc.scalar.copy(*b1)
         put_b(0)
-        nc.scalar.copy(b23[0][:], b23[1][:])
-        put_b(1)
-        put_b(2)
-        put_b(3)
-        nc.vector.tensor_copy(a0[0][:], a0[1][:])
-        nc.vector.tensor_copy(a1[0][:], a1[1][:])
+        nc.scalar.copy(*b23)
+        for t in range(1, PACK):
+            put_b(t)
+
+        nc.vector.tensor_copy(*a0)
+        nc.vector.tensor_copy(*a1)
         put_a(0)
         join(nc.gpsimd, 0)
-        nc.vector.tensor_copy(a23[0][:], a23[1][:])
+        nc.vector.tensor_copy(*a23)
         put_a(1)
         join(nc.gpsimd, 1)
         put_a(2)
         look(0, 0, O)
         join(nc.gpsimd, 2)
-        put_a(3)
+        put_a(LAST)
         look(1, 0, O)
         v_scale = sb([P, N], U8, "v_scale")
         nc.vector.tensor_copy(v_scale[:], vs_plane[:].indirect(output_list[:]))
-        join(nc.vector, 3)
+        join(nc.vector, LAST)
         look(2, 0, O)
         v_code = sb([P, N], U16, "v_code")
         nc.vector.tensor_copy(v_code[:], vs_table[:].indirect(output_list[:]))
 
-        for h in range(2):
-            look(3, h * HALF, (h + 1) * HALF)
-        out_banks = ("bank_b0", "bank_b1", "bank_y0", "bank_y1")
+        halves = [slice(h * HALF, (h + 1) * HALF) for h in range(2)]
+        for places in halves:
+            look(LAST, places.start, places.stop)
+
         hidden = []
-        for h in range(2):
-            cols = slice(h * HALF, (h + 1) * HALF)
+        for h, places in enumerate(halves):
             tile = sb([P, HALF, PACK], BF16, "hidden%d" % h)
             nc.vector.tensor_tensor(
-                tile[:].rearrange("p (c i) t -> p c t i", i=4),
-                values[:, :, cols].rearrange("p t (c i) -> p c t i", i=4),
-                gates[:, :, cols].rearrange("p t (c i) -> p c t i", i=4),
+                tile[:].rearrange("p (c i) t -> p c t i", i=RUN),
+                values[:, :, places].rearrange("p t (c i) -> p c t i", i=RUN),
+                gates[:, :, places].rearrange("p t (c i) -> p c t i", i=RUN),
                 ALU.mult,
             )
             hidden.append(tile)
-        for h in range(2):
-            cols = slice(h * HALF, (h + 1) * HALF)
+
+        out_banks = (("bank_b0", "bank_b1"), ("bank_y0", "bank_y1"))
+        movers = ((nc.scalar.copy, nc.scalar), (nc.vector.tensor_copy, nc.sync))
+        for h, places in enumerate(halves):
             h_code = sb([P, HALF], U32, "h_code%d" % h)
             h_scale = sb([P, HALF], U8, "h_scale%d" % h)
             nc.vector.quantize_mx(h_code[:].bitcast(E5M2), h_scale[:], hidden[h][:].rearrange("p o t -> p (o t)"))
-            for n in range(N // P):
-                rows = slice(n * P, (n + 1) * P)
-                bank = psum.tile([P, HALF], F32, name=out_banks[2 * h + n])
+            for n, (empty, queue) in enumerate(movers):
+                features = slice(n * P, (n + 1) * P)
+                bank = psum.tile([P, HALF], F32, name=out_banks[h][n])
                 nc.tensor.matmul_mx(
-                    bank[:], lhsT=v_code[:, rows].bitcast(E2M1), lhsT_scale=v_scale[:, rows],
+                    bank[:], lhsT=v_code[:, features].bitcast(E2M1), lhsT_scale=v_scale[:, features],
                     rhs=h_code[:].bitcast(E5M2), rhs_scale=h_scale[:], start=True, stop=True,
                 )
                 result = sb([P, HALF], F32, "result%d%d" % (h, n))
-                if n == 0:
-                    nc.scalar.copy(result[:], bank[:])
-                    nc.scalar.dma_start(out[rows, cols], result[:])
-                else:
-                    nc.vector.tensor_copy(result[:], bank[:])
-                    nc.sync.dma_start(out[rows, cols], result[:])
+                empty(result[:], bank[:])
+                queue.dma_start(out[features, places], result[:])

from contextlib import ExitStack

import concourse.mybir as mybir

K, T, J, R, V, C, O, N, S = 512, 1024, 256, 512, 1024, 512, 256, 256, 1024
FLOPS = 2 * K * R * J * 2 + 2 * R * N * O

F32 = mybir.dt.float32
BF16 = mybir.dt.bfloat16
I32 = mybir.dt.int32
U32 = mybir.dt.uint32
U16 = mybir.dt.uint16
U8 = mybir.dt.uint8
E4M3 = mybir.dt.float8_e4m3fn_x4
E5M2 = mybir.dt.float8_e5m2_x4
E2M1 = mybir.dt.float4_e2m1fn_x4
ACT = mybir.ActivationFunctionType
ALU = mybir.AluOpType

P = 128
PACK = 4
QUADS = 4
QUAD_ROWS = 4
PER_COLUMN = 16
RUN = 4
HALF = O // 2
LAST = PACK - 1


def tile_list_gatedshared_storeleads_store_plain_kernel(
    tc, xt_words, xt_scales, wt_words, wt_scales, w2_words, w2_scales, sa, sg, bg,
    vs_words, vs_scales, offs, offs2, offs3, offs4, offs5, offs6, offs7, out,
):
    nc = tc.nc
    with ExitStack() as ctx:
        keep = ctx.enter_context(tc.tile_pool(name="keep", bufs=1))
        psum = ctx.enter_context(tc.psum_pool(name="psum", bufs=1))

        def sb(shape, dtype, name):
            return keep.tile(shape, dtype, name=name, align_bytes=64)

        def load_list(src, name):
            tile = sb([P, src.shape[1]], U16, name)
            nc.sync.dma_start(tile[:], src)
            return tile

        def load_words(queue, src, shape, dtype, name):
            tile = sb(shape, dtype, name)
            queue.dma_start(tile[:].bitcast(I32), src.bitcast(I32))
            return tile

        def zeroed_plane(width, name):
            tile = sb([P, width], U8, name)
            nc.vector.memset(tile[:].bitcast(I32), 0)
            return tile

        def live_rows(plane, q):
            return plane[32 * q : 32 * q + QUAD_ROWS, :].bitcast(I32)

        def load_scales_in_place(queues, plane, src):
            for q, queue in enumerate(queues):
                queue.dma_start(live_rows(plane, q), src[0, QUAD_ROWS * q : QUAD_ROWS * (q + 1), :].bitcast(I32))

        def load_per_row(src, name):
            tile = sb([P, PACK], F32, name)
            nc.sync.dma_start(tile[:], src.rearrange("(p t) one -> p (t one)", t=PACK))
            return tile

        xt_plane = zeroed_plane(T, "xt_plane")
        w2_plane = zeroed_plane(R, "w2_plane")
        wt_plane = zeroed_plane(V, "wt_plane")
        vs_plane = zeroed_plane(S, "vs_plane")

        seed = sb([P, 1], F32, "seed")
        nc.gpsimd.memset(seed[:], 0.0)
        primer = sb([P, 1], F32, "primer")
        nc.scalar.activation(primer[:], seed[:], ACT.Sigmoid)

        w2_loaded = load_words(nc.scalar, w2_words[0].rearrange("p n t -> p (n t)"), [P, R], U32, "w2_loaded")
        xt_table = load_words(nc.scalar, xt_words[0], [P, T], U16, "xt_table")
        w2_staged = sb([QUAD_ROWS, QUADS, R], U8, "w2_staged")
        nc.sync.dma_start(
            w2_staged[:].bitcast(I32), w2_scales[0].rearrange("(q i) n -> i q n", i=QUAD_ROWS).bitcast(I32)
        )
        token_list = load_list(offs2, "token_list")
        load_scales_in_place([nc.sync, nc.scalar] * 2, xt_plane, xt_scales)
        wt_table = load_words(nc.sync, wt_words[0].rearrange("p n t -> p (n t)"), [P, V], U32, "wt_table")
        feature_list = load_list(offs, "feature_list")
        load_scales_in_place([nc.sync] * QUADS, wt_plane, wt_scales)
        b_places = load_list(offs4, "b_places")
        weight = load_per_row(sa, "weight")
        slope = load_per_row(sg, "slope")
        offset = load_per_row(bg, "offset")
        value_list = load_list(offs5, "value_list")
        gate_list = load_list(offs6, "gate_list")
        a_places = load_list(offs3, "a_places")
        output_list = load_list(offs7, "output_list")
        load_scales_in_place([nc.sync] * QUADS, vs_plane, vs_scales)
        vs_table = load_words(nc.sync, vs_words[0], [P, S], U16, "vs_table")

        for q in range(QUADS):
            nc.vector.tensor_copy(live_rows(w2_plane, q), w2_staged[:, q, :].bitcast(I32))
        w2_scale = sb([P, PACK, P], U8, "w2_scale")
        w2_plane_by_slice = w2_plane[:].rearrange("p (m t) -> p t m", t=PACK)
        nc.vector.tensor_copy(w2_scale[:, 0:2, :], w2_plane_by_slice[:, 0:2, :])
        nc.gpsimd.tensor_copy(w2_scale[:, 2:4, :], w2_plane_by_slice[:, 2:4, :])
        x_scale = sb([P, J], U8, "x_scale")
        nc.vector.tensor_copy(x_scale[:], xt_plane[:].indirect(token_list[:]))
        w2_code = sb([P, PACK, P], U32, "w2_code")
        for pair in (slice(0, 2), slice(2, 4)):
            nc.scalar.copy(
                w2_code[:, pair, :].rearrange("p t m -> p m t"),
                w2_loaded[:].rearrange("p (m t) -> p m t", t=PACK)[:, :, pair],
            )
        x_code = sb([P, J], U16, "x_code")
        nc.vector.tensor_copy(x_code[:], xt_table[:].indirect(token_list[:]))

        a_boards = [sb([P, C], F32, "a_board%d" % i) for i in range(2)]
        b_boards = [sb([P, C], F32, "b_board%d" % t) for t in range(PACK)]
        for board in b_boards[:2] + a_boards + b_boards[2:]:
            nc.vector.memset(board[:], 0.0)

        wt_code = sb([P, PACK, P], U32, "wt_code")
        wt_scale = sb([P, PACK, P], U8, "wt_scale")
        stationary = {"a": (wt_code, wt_scale, E4M3), "b": (w2_code, w2_scale, E5M2)}
        rows_of = {}

        def first_stage(which, *slices):
            name = "".join("%s%d" % (which, t) for t in slices)
            code, scale, fmt = stationary[which]
            bank = psum.tile([P, len(slices), J], F32, name="bank_" + name)
            rows = sb([P, len(slices), J], F32, "rows_" + name)
            for i, t in enumerate(slices):
                nc.tensor.matmul_mx(
                    bank[:, i, :], lhsT=code[:, t, :].bitcast(fmt), lhsT_scale=scale[:, t, :],
                    rhs=x_code[:].bitcast(E2M1), rhs_scale=x_scale[:], start=True, stop=True,
                )
                rows_of[which, t] = rows[:, i, :]
            return rows[:], bank[:]

        b0 = first_stage("b", 0)
        b1 = first_stage("b", 1)
        b23 = first_stage("b", 2, 3)
        nc.vector.tensor_copy(wt_code[:].rearrange("p t m -> p m t"), wt_table[:].indirect(feature_list[:]))
        nc.vector.tensor_copy(wt_scale[:].rearrange("p t m -> p m t"), wt_plane[:].indirect(feature_list[:]))
        a0 = first_stage("a", 0)
        a1 = first_stage("a", 1)
        a23 = first_stage("a", 2, 3)

        boards = [sb([P, C], F32, "board%d" % t) for t in range(LAST)]
        boards.append(boards[1])
        values = sb([P, PACK, O], F32, "values")
        gates = sb([P, PACK, O], F32, "gates")

        def put_b(t):
            nc.scalar.activation(b_boards[t][:].indirect(b_places[:]), rows_of["b", t], ACT.Copy)

        def put_a(t):
            nc.vector.tensor_copy(a_boards[t % 2][:].indirect(a_places[:]), rows_of["a", t])

        def join(engine, t):
            engine.tensor_tensor(boards[t][:], a_boards[t % 2][:], b_boards[t][:], ALU.add)

        def look(t, lo, hi):
            entries = slice(lo // PER_COLUMN, hi // PER_COLUMN)
            nc.scalar.activation(
                values[:, t, lo:hi], boards[t][:].indirect(value_list[:, entries]), ACT.Copy,
                scale=weight[:, t : t + 1],
            )
            nc.scalar.activation(
                gates[:, t, lo:hi], boards[t][:].indirect(gate_list[:, entries]), ACT.Sigmoid,
                bias=offset[:, t : t + 1], scale=slope[:, t : t + 1],
            )

        nc.scalar.copy(*b0)
        nc.scalar.copy(*b1)
        put_b(0)
        nc.scalar.copy(*b23)
        for t in range(1, PACK):
            put_b(t)

        nc.vector.tensor_copy(*a0)
        nc.vector.tensor_copy(*a1)
        put_a(0)
        join(nc.gpsimd, 0)
        nc.vector.tensor_copy(*a23)
        put_a(1)
        join(nc.gpsimd, 1)
        put_a(2)
        look(0, 0, O)
        join(nc.gpsimd, 2)
        put_a(LAST)
        look(1, 0, O)
        v_scale = sb([P, N], U8, "v_scale")
        nc.vector.tensor_copy(v_scale[:], vs_plane[:].indirect(output_list[:]))
        join(nc.vector, LAST)
        look(2, 0, O)
        v_code = sb([P, N], U16, "v_code")
        nc.vector.tensor_copy(v_code[:], vs_table[:].indirect(output_list[:]))

        halves = [slice(h * HALF, (h + 1) * HALF) for h in range(2)]
        for places in halves:
            look(LAST, places.start, places.stop)

        hidden = []
        for h, places in enumerate(halves):
            tile = sb([P, HALF, PACK], BF16, "hidden%d" % h)
            nc.vector.tensor_tensor(
                tile[:].rearrange("p (c i) t -> p c t i", i=RUN),
                values[:, :, places].rearrange("p t (c i) -> p c t i", i=RUN),
                gates[:, :, places].rearrange("p t (c i) -> p c t i", i=RUN),
                ALU.mult,
            )
            hidden.append(tile)

        out_banks = (("bank_b0", "bank_b1"), ("bank_y0", "bank_y1"))
        movers = ((nc.scalar.copy, nc.scalar), (nc.vector.tensor_copy, nc.sync))
        for h, places in enumerate(halves):
            h_code = sb([P, HALF], U32, "h_code%d" % h)
            h_scale = sb([P, HALF], U8, "h_scale%d" % h)
            nc.vector.quantize_mx(h_code[:].bitcast(E5M2), h_scale[:], hidden[h][:].rearrange("p o t -> p (o t)"))
            for n, (empty, queue) in enumerate(movers):
                features = slice(n * P, (n + 1) * P)
                bank = psum.tile([P, HALF], F32, name=out_banks[h][n])
                nc.tensor.matmul_mx(
                    bank[:], lhsT=v_code[:, features].bitcast(E2M1), lhsT_scale=v_scale[:, features],
                    rhs=h_code[:].bitcast(E5M2), rhs_scale=h_scale[:], start=True, stop=True,
                )
                result = sb([P, HALF], F32, "result%d%d" % (h, n))
                empty(result[:], bank[:])
                queue.dma_start(out[features, places], result[:])
